import numpy as np, ml_dtypes
CORES = [51,54,179,182]
N = 4
import mx_ref
NC = 128
A = np.float32(0.0125)
BF = ml_dtypes.bfloat16
def cut(t, i, w=512):
    return t[:, w * i:w * i + w]
def tile(rs):
    return np.stack(rs, axis=2).reshape(128, -1).astype(BF)
def pk(c, s, i=0):
    return (np.ascontiguousarray(c[:, 512 * i:512 * i + 512]), mx_ref.live(s[:, 128 * i:128 * i + 128]))
def raw(rng):
    def f(*shape):
        return mx_ref.flush((rng.standard_normal(shape, dtype=np.float32) * np.exp2(rng.integers(-2, 3, shape[:-1] + (1,)))).astype(BF))
    return {"q": f(N, 128, 4 * NC), "k": f(N, 128, 4 * 512), "v": f(N, 128, 512)}
def raw_blocks(rng):
    d = raw(rng)
    for k in ("v",): d[k] = mx_ref.spread(d[k], rng, 4)
    for k in ("q", "k"): d[k] = mx_ref.spread(d[k], rng, 1)
    return d
def raw_wide(rng):
    d = raw(rng)
    for k in ("v",): d[k] = mx_ref.flush((d[k].astype(np.float32) * np.exp2(rng.integers(-8, 9, (N, 1, 1))).astype(np.float32)).astype(BF))
    return d
def raw_sharp(rng):
    d = raw(rng); v = d["q"].astype(np.float32).reshape(N, 128, -1, 4)
    d["q"] = mx_ref.flush((v * np.exp2(rng.integers(-2, 4, (N, 1, v.shape[2], 1))).astype(np.float32)).reshape(d["q"].shape).astype(BF))
    return d
def raw_far(rng):
    d = raw(rng); d["q"] = (d["q"].astype(np.float32) * 10).astype(BF)
    return d
def raw_faroff(rng):
    d = raw(rng); v = d["k"].astype(np.float32).reshape(N, 128, -1, 4)
    d["k"] = mx_ref.flush((v + 192 * rng.standard_normal((1, 128, 1, 4), dtype=np.float32)).reshape(d["k"].shape).astype(BF))
    return d
def pack(d, rng):
    o = {"q": d["q"]}
    for m in ("k", "v"):
        t = d[m]; c = np.zeros(t.shape, np.uint8); s = np.zeros((N, 128, t.shape[2] // 4), np.uint8)
        for r in range(N):
            for i in range(t.shape[2] // 512):
                a, b = mx_ref.quantize(cut(t[r], i)); c[r][:, 512 * i:512 * i + 512] = a; s[r][:, 128 * i:128 * i + 128] = mx_ref.plane(b, rng)
        o[m + "c"], o[m + "s"] = c, s
    return o
def setup_inputs(rng):
    return pack(raw(rng), rng)
def setup_inputs_blocks(rng):
    return pack(raw_blocks(rng), rng)
def setup_inputs_far(rng):
    return pack(raw_far(rng), rng)
def setup_inputs_faroff(rng):
    return pack(raw_faroff(rng), rng)
def setup_inputs_sharp(rng):
    return pack(raw_sharp(rng), rng)
def setup_inputs_wide(rng):
    return pack(raw_wide(rng), rng)
def reference(q, kc, ks, vc, vs, own=None):
    ONE = mx_ref.quantize(np.ones((128, 512), BF))
    K = [[pk(kc[j], ks[j], b) for b in range(4)] for j in range(N)]; V = [pk(vc[j], vs[j]) for j in range(N)]
    Q = [mx_ref.quantize(q[i]) for i in range(N)]
    lo = np.zeros((N, N, NC), np.float32); w = lo.copy(); wlo = lo.copy(); whi = lo.copy(); p = np.zeros((N, N, 128, 4 * NC), BF); o = np.zeros((N, 128, NC), np.float32)
    S = [[[mx_ref.matmul(K[j][b], Q[i]) * A for b in range(4)] for i in range(N)] for j in range(N)]
    for j in range(N):
        lo[j] = [np.max(s, axis=(0, 1)) for s in S[j]]
    hi = np.broadcast_to(lo.max(axis=0) + 8, lo.shape).copy()
    c = lo if own is None else own["c"]
    for j in range(N):
        for i in range(N):
            p[j][i] = tile([np.exp(np.maximum(s - c[j][i], -20).astype(np.float64)).astype(np.float32) for s in S[j][i]])
    use = p if own is None else own["p"]
    for i in range(N):
        e = np.exp((c[:, i] - c[:, i].max(axis=0)).astype(np.float64)); wlo[i] = e * (1 - 4e-5); whi[i] = e * (1 + 4e-5)
        w[i] = e if own is None else own["w"][i]
        num = den = 0
        for j in range(N):
            P = mx_ref.quantize(use[j][i])
            num = num + w[i][j].astype(np.float64) * mx_ref.matmul(V[j], P); den = den + w[i][j].astype(np.float64) * mx_ref.matmul(ONE, P)
        o[i] = (num / den).astype(np.float32)
    return {"c": c, "c__lo": lo, "c__hi": hi, "p": p, "w": w, "w__lo": wlo, "w__hi": whi, "o": o}

@@ -1,0 +1,289 @@
+from concourse.bass import DstId, RemoteDMATransfer
+from concourse.mybir import dt, AluOpType, AxisListType, ActivationFunctionType
+
+N = 4
+W = 132
+SCALE = 0.0125
+F8 = "float8_e4m3fn_x4"
+
+SCRATCH = {
+    "qin": ("sbuf", [128, 512], "bfloat16"),
+    "ones": ("sbuf", [128, 512], "bfloat16"),
+    "kcs": ("sbuf", [128, 512], F8),
+    "kss": ("sbuf", [128, 512], "uint8"),
+    "vo": ("sbuf", [128, 256], F8),
+    "vos": ("sbuf", [128, 256], "uint8"),
+    "nm": ("sbuf", [128, 4], "float32"),
+    "nc": ("sbuf", [128, 4], "float32"),
+    "m20": ("sbuf", [128, 1], "float32"),
+    "e20": ("sbuf", [128, 1], "bfloat16"),
+    "rcv": ("sbuf", [128, N * W], "float32"),
+    "cw": ("sbuf", [128, 32], "float32"),
+    "cwt": ("sbuf", [32, 128], "float32"),
+    "low": ("sbuf", [128, 1], "float32"),
+    "den": ("sbuf", [128, 4], "float32"),
+    "rd": ("sbuf", [128, 1], "float32"),
+    "u": ("sbuf", [128, 512], "float32"),
+    "acc1": ("sbuf", [128, 128], "float32"),
+    "acc2": ("sbuf", [128, 128], "float32"),
+    "acc3": ("sbuf", [128, 128], "float32"),
+    "ot": ("sbuf", [128, 128], "float32"),
+    "oh": ("sbuf", [128, 64], "float32"),
+    "of": ("sbuf", [128, 128], "float32"),
+    "S": ("psum", [128, 2048], "float32"),
+    "A": ("psum", [128, 2048], "float32"),
+}
+SEMAPHORES = ["ldq", "ldk", "ldks", "ldv", "ldvs", "ones_set", "m20_set", "cw_set", "e20_set", "qq", "oneq", "loc",
+              "c3", "stp", "stc", "sto", "sto2", "cpos", "lows", "ws", "dens", "accs", "cwts", "rds", "ots", "ohs", "ofv", "ofa"]
+for _s in range(N):
+    SCRATCH["e%d" % _s] = ("sbuf", [128, 4, 128], "bfloat16")
+    SCRATCH["pt%d" % _s] = ("sbuf", [128, 4, 128], "bfloat16")
+    SCRATCH["tile%d" % _s] = ("sbuf", [128, 512], "bfloat16")
+    SCRATCH["qc%d" % _s] = ("sbuf", [128, 128], F8)
+    SCRATCH["qs%d" % _s] = ("sbuf", [128, 128], "uint8")
+    SCRATCH["pc%d" % _s] = ("sbuf", [128, 128], F8)
+    SCRATCH["ps%d" % _s] = ("sbuf", [128, 128], "uint8")
+    if _s:
+        SCRATCH["snd%d" % _s] = ("sbuf", [128, W], "float32")
+    SEMAPHORES += ["%s%d" % (_n, _s) for _n in ("q_in", "a_in", "mmS", "mmA", "red", "neg", "ex", "tr", "il", "qt", "ac", "us")]
+
+
+def rank_program(g, core, T, topo):
+    me = T.rank_of(core)
+    if me is None:
+        return
+    ACT = ActivationFunctionType
+    X = AxisListType.X
+    S = T.sem
+    ve, te, sc, sy = g.vector, g.tensor, g.scalar, g.sync
+    cores = list(T.cores)
+
+    def near(c):
+        return (topo.host(c), topo.chip(c)) == (topo.host(core), topo.chip(core))
+
+    order = sorted(range(N), key=lambda r: (r != me, not near(cores[r]), topo.die(cores[r]) != topo.die(core)))
+    dst = [cores[r] for r in order]
+    full = [0] + [topo.mask(core, d) for d in dst[1:]]
+    away = full[2]
+    here = full[1] & ~away
+
+    def count(m):
+        return bin(m).count("1")
+
+    def did(d):
+        rid, pid = topo.addr(d, core)
+        return DstId(rid=rid, pnc=pid)
+
+    def move(s, out, in_, sem, mask):
+        return RemoteDMATransfer(src=in_, dst=out, dst_ids=[did(dst[s])], dma_engine_mask=mask, remote_sem=sem)
+
+    def codes(t):
+        return t[:].bitcast(dt.uint8)
+
+    def slot(s):
+        return order[s] * W
+
+    sy.dma_start(T.qin[:], T.q[:]).then_inc(S.ldq, 16)
+    sy.dma_start(T.kcs[:].bitcast(dt.uint8), T.kc[:]).then_inc(S.ldk, 16)
+    sc.dma_start(T.kss[:], T.ks[:]).then_inc(S.ldks, 16)
+    sy.dma_start(T.vo[:, 0:128].bitcast(dt.uint8), T.vc[:]).then_inc(S.ldv, 16)
+    sy.dma_start(T.vos[:, 0:128], T.vs[:]).then_inc(S.ldvs, 16)
+
+    nloc = [0]
+
+    def sent(transfers, masks):
+        g.remote_dma_fused(transfers, local_sem=S.loc)
+        nloc[0] += sum(count(t) for t in masks)
+
+    g.wait_ge(S.qq, 1)
+    sent([move(2, codes(T.qc2), codes(T.qc0), S.q_in2, away), move(1, codes(T.qc1), codes(T.qc0), S.q_in1, here)], [away, here])
+    sent([move(2, T.qs2[:], T.qs0[:], S.q_in2, away), move(1, T.qs1[:], T.qs0[:], S.q_in1, here)], [away, here])
+    sent([move(3, codes(T.qc3), codes(T.qc0), S.q_in3, away)], [away])
+    sent([move(3, T.qs3[:], T.qs0[:], S.q_in3, away)], [away])
+    mine = me * W
+    g.wait_ge(S.ac1, 2)
+    sent([move(1, T.rcv[:, mine:mine + 130], T.snd1[:, 0:130], S.a_in1, full[1])], [full[1]])
+    g.wait_ge(S.neg3, 1)
+    sent([move(3, T.rcv[:, mine + 129:mine + 130], T.nc[:, order[3]:order[3] + 1], S.c3, away)], [away])
+    g.wait_ge(S.ac2, 2)
+    sent([move(2, T.rcv[:, mine:mine + 130], T.snd2[:, 0:130], S.a_in2, away)], [away])
+    g.wait_ge(S.ac3, 1)
+    sent([move(3, T.rcv[:, mine:mine + 129], T.snd3[:, 0:129], S.a_in3, away)], [away])
+    g.wait_ge(S.loc, nloc[0])
+    qn = [0, 2 * count(here), 2 * count(away), 2 * count(away)]
+    an = [0, count(full[1]), count(away), count(away)]
+
+    def scores(s):
+        if s:
+            te.wait_ge(S["q_in%d" % s], qn[s])
+        else:
+            te.wait_ge(S.qq, 1)
+            te.wait_ge(S.ldk, 16)
+            te.wait_ge(S.ldks, 16)
+        te.matmul_mx(T.S[:, 512 * s:512 * s + 512], T["qc%d" % s][:], T["qs%d" % s][:], T.kcs[:], T.kss[:],
+                     True, True).then_inc(S["mmS%d" % s], 1)
+
+    def values(s):
+        if s == 0:
+            te.wait_ge(S.oneq, 1)
+            te.wait_ge(S.ldv, 16)
+            te.wait_ge(S.ldvs, 16)
+        te.wait_ge(S["qt%d" % s], 1)
+        te.matmul_mx(T.A[:, 512 * s:512 * s + 256], T["pc%d" % s][:], T["ps%d" % s][:], T.vo[:], T.vos[:],
+                     True, True).then_inc(S["mmA%d" % s], 1)
+
+    scores(0)
+    scores(1)
+    values(0)
+    scores(2)
+    scores(3)
+    values(1)
+    values(2)
+    values(3)
+
+    def expo(s):
+        r = order[s]
+        sc.wait_ge(S["neg%d" % s], 1)
+        sc.activation(T["e%d" % s][:], T.S[:, 512 * s:512 * s + 512], ACT.Exp, bias=T.nc[:, r:r + 1],
+                      scale=SCALE).then_inc(S["ex%d" % s], 1)
+        if s == 0:
+            sc.activation(T.rcv[:, slot(0) + 129:slot(0) + 130], T.nc[:, r:r + 1], ACT.Copy).then_inc(S.ac0, 1)
+        elif s < 3:
+            sc.activation(T["snd%d" % s][:, 129:130], T.nc[:, r:r + 1], ACT.Copy).then_inc(S["ac%d" % s], 1)
+
+    def leave(s):
+        sc.wait_ge(S["mmA%d" % s], 1)
+        out = T["snd%d" % s][:, 0:129] if s else T.rcv[:, slot(0):slot(0) + 129]
+        sc.activation(out, T.A[:, 512 * s:512 * s + 129], ACT.Copy).then_inc(S["ac%d" % s], 1)
+
+    sc.wait_ge(S.m20_set, 1)
+    sc.activation(T.e20[:], T.m20[:], ACT.Exp).then_inc(S.e20_set, 1)
+    expo(0)
+    leave(0)
+    expo(1)
+    expo(2)
+    leave(1)
+    expo(3)
+    sc.wait_ge(S.cw_set, 1)
+    sc.activation(T.cw[:, 0:4], T.nc[:, 0:4], ACT.Copy, scale=-1.0).then_inc(S.cpos, 1)
+    leave(2)
+    leave(3)
+
+    ve.memset(T.m20[:], -20.0).then_inc(S.m20_set, 1)
+    ve.memset(T.ones[:], 1.0).then_inc(S.ones_set, 1)
+    ve.memset(T.cw[:], 0.0).then_inc(S.cw_set, 1)
+    ve.wait_ge(S.ldq, 16)
+    ve.quantize_mx(T.qc0[:], T.qs0[:], T.qin[:]).then_inc(S.qq, 1)
+    ve.wait_ge(S.ones_set, 1)
+    ve.quantize_mx(T.vo[:, 128:256], T.vos[:, 128:256], T.ones[:]).then_inc(S.oneq, 1)
+
+    def top(s):
+        r = order[s]
+        ve.wait_ge(S["mmS%d" % s], 1)
+        ve.tensor_reduce(T.nm[:, r:r + 1], T.S[:, 512 * s:512 * s + 512], X, AluOpType.max,
+                         negate=True).then_inc(S["red%d" % s], 1)
+        ve.wait_ge(S["red%d" % s], 1)
+        ve.tensor_scalar(T.nc[:, r:r + 1], T.nm[:, r:r + 1], SCALE, None, AluOpType.mult).then_inc(S["neg%d" % s], 1)
+
+    def turn(s):
+        e, p = T["e%d" % s], T["pt%d" % s]
+        ve.wait_ge(S["ex%d" % s], 1)
+        for d in range(4):
+            for a in range(4):
+                ve.transpose(p[32 * d:32 * d + 32, :, 32 * a:32 * a + 32],
+                             e[32 * a:32 * a + 32, :, 32 * d:32 * d + 32]).then_inc(S["tr%d" % s], 1)
+        if s == 0:
+            ve.wait_ge(S.e20_set, 1)
+        ve.wait_ge(S["tr%d" % s], 16)
+        for b in range(4):
+            ve.tensor_scalar(T["tile%d" % s][:, b:512:4], p[:, b, :], T.e20[:, 0:1], None, AluOpType.max).then_inc(S["il%d" % s], 1)
+        ve.wait_ge(S["il%d" % s], 4)
+        ve.quantize_mx(T["pc%d" % s][:], T["ps%d" % s][:], T["tile%d" % s][:]).then_inc(S["qt%d" % s], 1)
+
+    top(0)
+    turn(0)
+    top(1)
+    top(2)
+    turn(1)
+    top(3)
+    turn(2)
+    turn(3)
+
+    ve.wait_ge(S.c3, count(away))
+    ve.wait_ge(S.ac0, 2)
+    ve.wait_ge(S.a_in1, an[1])
+    ve.wait_ge(S.a_in2, an[2])
+    ve.tensor_reduce(T.low[:], T.rcv[:, 129:N * W:W], X, AluOpType.min).then_inc(S.lows, 1)
+
+    def w(s):
+        return T.cw[:, 4 + order[s]:5 + order[s]]
+
+    def arr(s):
+        return T.rcv[:, slot(s):slot(s) + 128]
+
+    def tot(s):
+        return T.rcv[:, slot(s) + 128:slot(s) + 129]
+
+    def u(s):
+        return T.u[:, 128 * s:128 * s + 128]
+
+    sc.wait_ge(S.lows, 1)
+    sc.activation(T.cw[:, 4:8], T.rcv[:, 129:N * W:W], ACT.Exp, bias=T.low[:], scale=-1.0).then_inc(S.ws, 1)
+    sc.wait_ge(S.ws, 1)
+    for s in range(3):
+        sc.activation(u(s), arr(s), ACT.Identity, scale=w(s)).then_inc(S["us%d" % s], 1)
+    sc.wait_ge(S.a_in3, an[3])
+    sc.activation(u(3), arr(3), ACT.Identity, scale=w(3)).then_inc(S.us3, 1)
+
+    ve.wait_ge(S.ws, 1)
+    ve.tensor_scalar(T.den[:, 0:1], tot(0), w(0), None, AluOpType.mult).then_inc(S.dens, 1)
+    ve.wait_ge(S.cpos, 1)
+    for a in range(4):
+        ve.transpose(T.cwt[0:32, 32 * a:32 * a + 32], T.cw[32 * a:32 * a + 32, 0:32]).then_inc(S.cwts, 1)
+    for s in (1, 2):
+        ve.wait_ge(S.dens, s)
+        ve.tensor_scalar(T.den[:, s:s + 1], tot(s), w(s), T.den[:, s - 1:s], AluOpType.mult, AluOpType.add).then_inc(S.dens, 1)
+    ve.wait_ge(S.us0, 1)
+    ve.wait_ge(S.us1, 1)
+    ve.tensor_tensor(T.acc1[:], u(0), u(1), AluOpType.add).then_inc(S.accs, 1)
+    ve.wait_ge(S.us2, 1)
+    ve.wait_ge(S.accs, 1)
+    ve.tensor_tensor(T.acc2[:], T.acc1[:], u(2), AluOpType.add).then_inc(S.accs, 1)
+
+    ve.wait_ge(S.dens, 3)
+    ve.wait_ge(S.a_in3, an[3])
+    ve.tensor_scalar(T.den[:, 3:4], tot(3), w(3), T.den[:, 2:3], AluOpType.mult, AluOpType.add).then_inc(S.dens, 1)
+    ve.wait_ge(S.dens, 4)
+    ve.reciprocal(T.rd[:], T.den[:, 3:4]).then_inc(S.rds, 1)
+    ve.wait_ge(S.us3, 1)
+    ve.wait_ge(S.accs, 2)
+    ve.tensor_tensor(T.acc3[:], T.acc2[:], u(3), AluOpType.add).then_inc(S.accs, 1)
+    ve.wait_ge(S.rds, 1)
+    ve.wait_ge(S.accs, 3)
+    ve.tensor_scalar(T.ot[:], T.acc3[:], T.rd[:], None, AluOpType.mult).then_inc(S.ots, 1)
+    ve.wait_ge(S.ots, 1)
+    ve.transpose(T.oh[:], T.ot[:, 64:128]).then_inc(S.ohs, 1)
+    for d in (0, 1):
+        for a in range(4):
+            ve.transpose(T.of[32 * d:32 * d + 32, 32 * a:32 * a + 32],
+                         T.ot[32 * a:32 * a + 32, 32 * d:32 * d + 32]).then_inc(S.ofv, 1)
+    sc.wait_ge(S.ohs, 1)
+    for d in (2, 3):
+        for a in range(4):
+            sc.activation(T.of[32 * d:32 * d + 32, 32 * a:32 * a + 32],
+                          T.oh[32 * a:32 * a + 32, 32 * (d - 2):32 * (d - 2) + 32], ACT.Copy).then_inc(S.ofa, 1)
+
+    for s in range(4):
+        sy.wait_ge(S["il%d" % s], 4)
+        sy.dma_start(T.p[order[s]], T["tile%d" % s][:]).then_inc(S.stp, 16)
+    sy.wait_ge(S.cwts, 4)
+    sy.dma_start(T.c[:], T.cwt[0:4, :]).then_inc(S.stc, 16)
+    sy.dma_start(T.w[:], T.cwt[4:8, :]).then_inc(S.stc, 16)
+    sy.wait_ge(S.ofv, 8)
+    sy.dma_start(T.o[0:64, :], T.of[0:64, :]).then_inc(S.sto, 16)
+    sc.wait_ge(S.ofa, 8)
+    sc.dma_start(T.o[64:128, :], T.of[64:128, :]).then_inc(S.sto2, 16)
+    sc.wait_ge(S.sto2, 16)
+    sy.wait_ge(S.stp, 64)
+    sy.wait_ge(S.stc, 32)
+    sy.wait_ge(S.sto, 16)

@@ -34,7 +34,7 @@ SCRATCH = {
     "A": ("psum", [128, 2048], "float32"),
 }
 SEMAPHORES = ["ldq", "ldk", "ldks", "ldv", "ldvs", "ones_set", "m20_set", "cw_set", "e20_set", "qq", "oneq", "loc",
-              "c3", "stp", "stc", "sto", "sto2", "cpos", "lows", "ws", "dens", "accs", "cwts", "rds", "ots", "ohs", "ofv", "ofa"]
+              "c1", "c3", "stp", "stc", "sto", "sto2", "cpos", "lows", "ws", "dens", "accs", "cwts", "rds", "ots", "ohs", "ofv", "ofa"]
 for _s in range(N):
     SCRATCH["e%d" % _s] = ("sbuf", [128, 4, 128], "bfloat16")
     SCRATCH["pt%d" % _s] = ("sbuf", [128, 4, 128], "bfloat16")
@@ -83,9 +83,12 @@ def rank_program(g, core, T, topo):
     def slot(s):
         return order[s] * W
 
+    def neg(s):
+        return T.nc[:, order[s]:order[s] + 1]
+
     sy.dma_start(T.qin[:], T.q[:]).then_inc(S.ldq, 16)
     sy.dma_start(T.kcs[:].bitcast(dt.uint8), T.kc[:]).then_inc(S.ldk, 16)
-    sc.dma_start(T.kss[:], T.ks[:]).then_inc(S.ldks, 16)
+    sy.dma_start(T.kss[:], T.ks[:]).then_inc(S.ldks, 16)
     sy.dma_start(T.vo[:, 0:128].bitcast(dt.uint8), T.vc[:]).then_inc(S.ldv, 16)
     sy.dma_start(T.vos[:, 0:128], T.vs[:]).then_inc(S.ldvs, 16)
 
@@ -101,14 +104,16 @@ def rank_program(g, core, T, topo):
     sent([move(3, codes(T.qc3), codes(T.qc0), S.q_in3, away)], [away])
     sent([move(3, T.qs3[:], T.qs0[:], S.q_in3, away)], [away])
     mine = me * W
-    g.wait_ge(S.ac1, 2)
-    sent([move(1, T.rcv[:, mine:mine + 130], T.snd1[:, 0:130], S.a_in1, full[1])], [full[1]])
+    g.wait_ge(S.neg1, 1)
     g.wait_ge(S.neg3, 1)
-    sent([move(3, T.rcv[:, mine + 129:mine + 130], T.nc[:, order[3]:order[3] + 1], S.c3, away)], [away])
+    cme = T.rcv[:, mine + 129:mine + 130]
+    sent([move(3, cme, neg(3), S.c3, away), move(1, cme, neg(1), S.c1, here)], [away, here])
     g.wait_ge(S.ac2, 2)
     sent([move(2, T.rcv[:, mine:mine + 130], T.snd2[:, 0:130], S.a_in2, away)], [away])
     g.wait_ge(S.ac3, 1)
     sent([move(3, T.rcv[:, mine:mine + 129], T.snd3[:, 0:129], S.a_in3, away)], [away])
+    g.wait_ge(S.ac1, 1)
+    sent([move(1, T.rcv[:, mine:mine + 129], T.snd1[:, 0:129], S.a_in1, full[1])], [full[1]])
     g.wait_ge(S.loc, nloc[0])
     qn = [0, 2 * count(here), 2 * count(away), 2 * count(away)]
     an = [0, count(full[1]), count(away), count(away)]
@@ -133,23 +138,18 @@ def rank_program(g, core, T, topo):
                      True, True).then_inc(S["mmA%d" % s], 1)
 
     scores(0)
+    scores(2)
     scores(1)
     values(0)
-    scores(2)
     scores(3)
-    values(1)
     values(2)
     values(3)
+    values(1)
 
     def expo(s):
-        r = order[s]
         sc.wait_ge(S["neg%d" % s], 1)
-        sc.activation(T["e%d" % s][:], T.S[:, 512 * s:512 * s + 512], ACT.Exp, bias=T.nc[:, r:r + 1],
+        sc.activation(T["e%d" % s][:], T.S[:, 512 * s:512 * s + 512], ACT.Exp, bias=neg(s),
                       scale=SCALE).then_inc(S["ex%d" % s], 1)
-        if s == 0:
-            sc.activation(T.rcv[:, slot(0) + 129:slot(0) + 130], T.nc[:, r:r + 1], ACT.Copy).then_inc(S.ac0, 1)
-        elif s < 3:
-            sc.activation(T["snd%d" % s][:, 129:130], T.nc[:, r:r + 1], ACT.Copy).then_inc(S["ac%d" % s], 1)
 
     def leave(s):
         sc.wait_ge(S["mmA%d" % s], 1)
@@ -159,15 +159,17 @@ def rank_program(g, core, T, topo):
     sc.wait_ge(S.m20_set, 1)
     sc.activation(T.e20[:], T.m20[:], ACT.Exp).then_inc(S.e20_set, 1)
     expo(0)
+    sc.activation(T.rcv[:, slot(0) + 129:slot(0) + 130], neg(0), ACT.Copy).then_inc(S.ac0, 1)
     leave(0)
-    expo(1)
     expo(2)
-    leave(1)
+    expo(1)
+    sc.activation(T.snd2[:, 129:130], neg(2), ACT.Copy).then_inc(S.ac2, 1)
     expo(3)
     sc.wait_ge(S.cw_set, 1)
     sc.activation(T.cw[:, 0:4], T.nc[:, 0:4], ACT.Copy, scale=-1.0).then_inc(S.cpos, 1)
     leave(2)
     leave(3)
+    leave(1)
 
     ve.memset(T.m20[:], -20.0).then_inc(S.m20_set, 1)
     ve.memset(T.ones[:], 1.0).then_inc(S.ones_set, 1)
@@ -182,38 +184,59 @@ def rank_program(g, core, T, topo):
         ve.wait_ge(S["mmS%d" % s], 1)
         ve.tensor_reduce(T.nm[:, r:r + 1], T.S[:, 512 * s:512 * s + 512], X, AluOpType.max,
                          negate=True).then_inc(S["red%d" % s], 1)
-        ve.wait_ge(S["red%d" % s], 1)
-        ve.tensor_scalar(T.nc[:, r:r + 1], T.nm[:, r:r + 1], SCALE, None, AluOpType.mult).then_inc(S["neg%d" % s], 1)
 
-    def turn(s):
+    def shift(s):
+        r = order[s]
+        ve.wait_ge(S["red%d" % s], 1)
+        ve.tensor_scalar(neg(s), T.nm[:, r:r + 1], SCALE, None, AluOpType.mult).then_inc(S["neg%d" % s], 1)
+
+    def turn(s, lo, hi):
         e, p = T["e%d" % s], T["pt%d" % s]
-        ve.wait_ge(S["ex%d" % s], 1)
-        for d in range(4):
-            for a in range(4):
-                ve.transpose(p[32 * d:32 * d + 32, :, 32 * a:32 * a + 32],
-                             e[32 * a:32 * a + 32, :, 32 * d:32 * d + 32]).then_inc(S["tr%d" % s], 1)
+        if lo == 0:
+            ve.wait_ge(S["ex%d" % s], 1)
+        for x in range(lo, hi):
+            d, a = x // 4, x % 4
+            ve.transpose(p[32 * d:32 * d + 32, :, 32 * a:32 * a + 32],
+                         e[32 * a:32 * a + 32, :, 32 * d:32 * d + 32]).then_inc(S["tr%d" % s], 1)
+
+    def weave(s):
         if s == 0:
             ve.wait_ge(S.e20_set, 1)
         ve.wait_ge(S["tr%d" % s], 16)
         for b in range(4):
-            ve.tensor_scalar(T["tile%d" % s][:, b:512:4], p[:, b, :], T.e20[:, 0:1], None, AluOpType.max).then_inc(S["il%d" % s], 1)
+            ve.tensor_scalar(T["tile%d" % s][:, b:512:4], T["pt%d" % s][:, b, :], T.e20[:, 0:1], None,
+                             AluOpType.max).then_inc(S["il%d" % s], 1)
+
+    def pack(s):
         ve.wait_ge(S["il%d" % s], 4)
         ve.quantize_mx(T["pc%d" % s][:], T["ps%d" % s][:], T["tile%d" % s][:]).then_inc(S["qt%d" % s], 1)
 
     top(0)
-    turn(0)
-    top(1)
+    shift(0)
+    turn(0, 0, 16)
+    weave(0)
+    pack(0)
     top(2)
-    turn(1)
+    shift(2)
+    top(1)
+    shift(1)
+    turn(2, 0, 8)
     top(3)
-    turn(2)
-    turn(3)
-
-    ve.wait_ge(S.c3, count(away))
-    ve.wait_ge(S.ac0, 2)
-    ve.wait_ge(S.a_in1, an[1])
-    ve.wait_ge(S.a_in2, an[2])
-    ve.tensor_reduce(T.low[:], T.rcv[:, 129:N * W:W], X, AluOpType.min).then_inc(S.lows, 1)
+    turn(2, 8, 12)
+    shift(3)
+    turn(2, 12, 16)
+    turn(1, 0, 4)
+    weave(2)
+    turn(1, 4, 6)
+    pack(2)
+    turn(3, 0, 16)
+    turn(1, 6, 10)
+    weave(3)
+    turn(1, 10, 12)
+    pack(3)
+    turn(1, 12, 16)
+    weave(1)
+    pack(1)
 
     def w(s):
         return T.cw[:, 4 + order[s]:5 + order[s]]
@@ -227,37 +250,46 @@ def rank_program(g, core, T, topo):
     def u(s):
         return T.u[:, 128 * s:128 * s + 128]
 
+    shifts = T.rcv[:, 129:N * W:W]
+    ve.wait_ge(S.c1, count(here))
+    ve.wait_ge(S.c3, count(away))
+    ve.wait_ge(S.ac0, 2)
+    ve.wait_ge(S.a_in2, an[2])
+    ve.tensor_reduce(T.low[:], shifts, X, AluOpType.min).then_inc(S.lows, 1)
+
     sc.wait_ge(S.lows, 1)
-    sc.activation(T.cw[:, 4:8], T.rcv[:, 129:N * W:W], ACT.Exp, bias=T.low[:], scale=-1.0).then_inc(S.ws, 1)
+    sc.activation(T.cw[:, 4:8], shifts, ACT.Exp, bias=T.low[:], scale=-1.0).then_inc(S.ws, 1)
     sc.wait_ge(S.ws, 1)
-    for s in range(3):
+    for s in (0, 2, 3, 1):
+        if s in (1, 3):
+            sc.wait_ge(S["a_in%d" % s], an[s])
         sc.activation(u(s), arr(s), ACT.Identity, scale=w(s)).then_inc(S["us%d" % s], 1)
-    sc.wait_ge(S.a_in3, an[3])
-    sc.activation(u(3), arr(3), ACT.Identity, scale=w(3)).then_inc(S.us3, 1)
 
     ve.wait_ge(S.ws, 1)
     ve.tensor_scalar(T.den[:, 0:1], tot(0), w(0), None, AluOpType.mult).then_inc(S.dens, 1)
     ve.wait_ge(S.cpos, 1)
     for a in range(4):
         ve.transpose(T.cwt[0:32, 32 * a:32 * a + 32], T.cw[32 * a:32 * a + 32, 0:32]).then_inc(S.cwts, 1)
-    for s in (1, 2):
-        ve.wait_ge(S.dens, s)
-        ve.tensor_scalar(T.den[:, s:s + 1], tot(s), w(s), T.den[:, s - 1:s], AluOpType.mult, AluOpType.add).then_inc(S.dens, 1)
+    ve.wait_ge(S.dens, 1)
+    ve.tensor_scalar(T.den[:, 1:2], tot(2), w(2), T.den[:, 0:1], AluOpType.mult, AluOpType.add).then_inc(S.dens, 1)
     ve.wait_ge(S.us0, 1)
-    ve.wait_ge(S.us1, 1)
-    ve.tensor_tensor(T.acc1[:], u(0), u(1), AluOpType.add).then_inc(S.accs, 1)
     ve.wait_ge(S.us2, 1)
+    ve.tensor_tensor(T.acc1[:], u(0), u(2), AluOpType.add).then_inc(S.accs, 1)
+    ve.wait_ge(S.a_in3, an[3])
+    ve.wait_ge(S.dens, 2)
+    ve.tensor_scalar(T.den[:, 2:3], tot(3), w(3), T.den[:, 1:2], AluOpType.mult, AluOpType.add).then_inc(S.dens, 1)
+    ve.wait_ge(S.us3, 1)
     ve.wait_ge(S.accs, 1)
-    ve.tensor_tensor(T.acc2[:], T.acc1[:], u(2), AluOpType.add).then_inc(S.accs, 1)
+    ve.tensor_tensor(T.acc2[:], T.acc1[:], u(3), AluOpType.add).then_inc(S.accs, 1)
 
     ve.wait_ge(S.dens, 3)
-    ve.wait_ge(S.a_in3, an[3])
-    ve.tensor_scalar(T.den[:, 3:4], tot(3), w(3), T.den[:, 2:3], AluOpType.mult, AluOpType.add).then_inc(S.dens, 1)
+    ve.wait_ge(S.a_in1, an[1])
+    ve.tensor_scalar(T.den[:, 3:4], tot(1), w(1), T.den[:, 2:3], AluOpType.mult, AluOpType.add).then_inc(S.dens, 1)
     ve.wait_ge(S.dens, 4)
     ve.reciprocal(T.rd[:], T.den[:, 3:4]).then_inc(S.rds, 1)
-    ve.wait_ge(S.us3, 1)
+    ve.wait_ge(S.us1, 1)
     ve.wait_ge(S.accs, 2)
-    ve.tensor_tensor(T.acc3[:], T.acc2[:], u(3), AluOpType.add).then_inc(S.accs, 1)
+    ve.tensor_tensor(T.acc3[:], T.acc2[:], u(1), AluOpType.add).then_inc(S.accs, 1)
     ve.wait_ge(S.rds, 1)
     ve.wait_ge(S.accs, 3)
     ve.tensor_scalar(T.ot[:], T.acc3[:], T.rd[:], None, AluOpType.mult).then_inc(S.ots, 1)
@@ -273,12 +305,15 @@ def rank_program(g, core, T, topo):
             sc.activation(T.of[32 * d:32 * d + 32, 32 * a:32 * a + 32],
                           T.oh[32 * a:32 * a + 32, 32 * (d - 2):32 * (d - 2) + 32], ACT.Copy).then_inc(S.ofa, 1)
 
-    for s in range(4):
+    for s in (0, 2, 3):
         sy.wait_ge(S["il%d" % s], 4)
         sy.dma_start(T.p[order[s]], T["tile%d" % s][:]).then_inc(S.stp, 16)
     sy.wait_ge(S.cwts, 4)
     sy.dma_start(T.c[:], T.cwt[0:4, :]).then_inc(S.stc, 16)
     sy.dma_start(T.w[:], T.cwt[4:8, :]).then_inc(S.stc, 16)
+    sy.wait_ge(S.a_in1, an[1])
+    sy.wait_ge(S.il1, 4)
+    sy.dma_start(T.p[order[1]], T.tile1[:]).then_inc(S.stp, 16)
     sy.wait_ge(S.ofv, 8)
     sy.dma_start(T.o[0:64, :], T.of[0:64, :]).then_inc(S.sto, 16)
     sc.wait_ge(S.ofa, 8)

@@ -28,16 +28,21 @@ SCRATCH = {
     "acc2": ("sbuf", [128, 128], "float32"),
     "acc3": ("sbuf", [128, 128], "float32"),
     "ot": ("sbuf", [128, 128], "float32"),
-    "oh": ("sbuf", [128, 64], "float32"),
-    "of": ("sbuf", [128, 128], "float32"),
+    "oh": ("sbuf", [128, 2, 64], "float32"),
+    "of": ("sbuf", [128, 2, 2, 32], "float32"),
+    "e1": ("sbuf", [128, 4, 4, 32], "bfloat16"),
+    "et1": ("sbuf", [128, 4, 128], "bfloat16"),
+    "pt1": ("sbuf", [128, 4, 128], "bfloat16"),
     "S": ("psum", [128, 2048], "float32"),
     "A": ("psum", [128, 2048], "float32"),
 }
-SEMAPHORES = ["ldq", "ldk", "ldks", "ldv", "ldvs", "ones_set", "m20_set", "cw_set", "e20_set", "qq", "oneq", "loc",
-              "c1", "c3", "stp", "stc", "sto", "sto2", "cpos", "lows", "ws", "dens", "accs", "cwts", "rds", "ots", "ohs", "ofv", "ofa"]
+SEMAPHORES = ["ldq", "ldk", "ldks", "ldv", "ldvs", "ones_set", "m20_set", "cw_set", "e20_set", "qq", "oneq", "loc", "locm",
+              "c1", "c3", "stp", "stc", "sto", "sto2", "cpos", "lows", "ws", "dens", "accs", "ah0", "ah1", "cwts", "rds", "ots",
+              "ota", "xd", "oh0", "oh1", "of0", "of1", "oa0", "oa1"]
 for _s in range(N):
-    SCRATCH["e%d" % _s] = ("sbuf", [128, 4, 128], "bfloat16")
-    SCRATCH["pt%d" % _s] = ("sbuf", [128, 4, 128], "bfloat16")
+    if _s != 1:
+        SCRATCH["e%d" % _s] = ("sbuf", [128, 4, 128], "bfloat16")
+        SCRATCH["pt%d" % _s] = ("sbuf", [128, 4, 128], "bfloat16")
     SCRATCH["tile%d" % _s] = ("sbuf", [128, 512], "bfloat16")
     SCRATCH["qc%d" % _s] = ("sbuf", [128, 128], F8)
     SCRATCH["qs%d" % _s] = ("sbuf", [128, 128], "uint8")
@@ -87,22 +92,21 @@ def rank_program(g, core, T, topo):
         return T.nc[:, order[s]:order[s] + 1]
 
     sy.dma_start(T.qin[:], T.q[:]).then_inc(S.ldq, 16)
-    sy.dma_start(T.kcs[:].bitcast(dt.uint8), T.kc[:]).then_inc(S.ldk, 16)
+    sc.dma_start(T.kcs[:].bitcast(dt.uint8), T.kc[:]).then_inc(S.ldk, 16)
     sy.dma_start(T.kss[:], T.ks[:]).then_inc(S.ldks, 16)
-    sy.dma_start(T.vo[:, 0:128].bitcast(dt.uint8), T.vc[:]).then_inc(S.ldv, 16)
-    sy.dma_start(T.vos[:, 0:128], T.vs[:]).then_inc(S.ldvs, 16)
 
-    nloc = [0]
+    nloc = {"q": 0, "m": 0}
 
-    def sent(transfers, masks):
-        g.remote_dma_fused(transfers, local_sem=S.loc)
-        nloc[0] += sum(count(t) for t in masks)
+    def sent(transfers, masks, kind="m"):
+        g.remote_dma_fused(transfers, local_sem=S.loc if kind == "q" else S.locm)
+        nloc[kind] += sum(count(t) for t in masks)
 
     g.wait_ge(S.qq, 1)
-    sent([move(2, codes(T.qc2), codes(T.qc0), S.q_in2, away), move(1, codes(T.qc1), codes(T.qc0), S.q_in1, here)], [away, here])
-    sent([move(2, T.qs2[:], T.qs0[:], S.q_in2, away), move(1, T.qs1[:], T.qs0[:], S.q_in1, here)], [away, here])
-    sent([move(3, codes(T.qc3), codes(T.qc0), S.q_in3, away)], [away])
-    sent([move(3, T.qs3[:], T.qs0[:], S.q_in3, away)], [away])
+    sent([move(2, codes(T.qc2), codes(T.qc0), S.q_in2, away)], [away], "q")
+    sent([move(1, codes(T.qc1), codes(T.qc0), S.q_in1, here)], [here], "q")
+    sent([move(2, T.qs2[:], T.qs0[:], S.q_in2, away), move(1, T.qs1[:], T.qs0[:], S.q_in1, here)], [away, here], "q")
+    sent([move(3, codes(T.qc3), codes(T.qc0), S.q_in3, away)], [away], "q")
+    sent([move(3, T.qs3[:], T.qs0[:], S.q_in3, away)], [away], "q")
     mine = me * W
     g.wait_ge(S.neg1, 1)
     g.wait_ge(S.neg3, 1)
@@ -113,10 +117,11 @@ def rank_program(g, core, T, topo):
     g.wait_ge(S.ac3, 1)
     sent([move(3, T.rcv[:, mine:mine + 129], T.snd3[:, 0:129], S.a_in3, away)], [away])
     g.wait_ge(S.ac1, 1)
-    sent([move(1, T.rcv[:, mine:mine + 129], T.snd1[:, 0:129], S.a_in1, full[1])], [full[1]])
-    g.wait_ge(S.loc, nloc[0])
+    sent([move(1, T.rcv[:, mine:mine + 129], T.snd1[:, 0:129], S.a_in1, here)], [here])
+    g.wait_ge(S.loc, nloc["q"])
+    g.wait_ge(S.locm, nloc["m"])
     qn = [0, 2 * count(here), 2 * count(away), 2 * count(away)]
-    an = [0, count(full[1]), count(away), count(away)]
+    an = [0, count(here), count(away), count(away)]
 
     def scores(s):
         if s:
@@ -138,10 +143,10 @@ def rank_program(g, core, T, topo):
                      True, True).then_inc(S["mmA%d" % s], 1)
 
     scores(0)
-    scores(2)
     scores(1)
-    values(0)
+    scores(2)
     scores(3)
+    values(0)
     values(2)
     values(3)
     values(1)
@@ -160,16 +165,15 @@ def rank_program(g, core, T, topo):
     sc.activation(T.e20[:], T.m20[:], ACT.Exp).then_inc(S.e20_set, 1)
     expo(0)
     sc.activation(T.rcv[:, slot(0) + 129:slot(0) + 130], neg(0), ACT.Copy).then_inc(S.ac0, 1)
-    leave(0)
-    expo(2)
     expo(1)
+    expo(2)
     sc.activation(T.snd2[:, 129:130], neg(2), ACT.Copy).then_inc(S.ac2, 1)
     expo(3)
-    sc.wait_ge(S.cw_set, 1)
-    sc.activation(T.cw[:, 0:4], T.nc[:, 0:4], ACT.Copy, scale=-1.0).then_inc(S.cpos, 1)
     leave(2)
     leave(3)
-    leave(1)
+    leave(0)
+    sc.wait_ge(S.cw_set, 1)
+    sc.activation(T.cw[:, 0:4], T.nc[:, 0:4], ACT.Copy, scale=-1.0).then_inc(S.cpos, 1)
 
     ve.memset(T.m20[:], -20.0).then_inc(S.m20_set, 1)
     ve.memset(T.ones[:], 1.0).then_inc(S.ones_set, 1)
@@ -199,12 +203,21 @@ def rank_program(g, core, T, topo):
             ve.transpose(p[32 * d:32 * d + 32, :, 32 * a:32 * a + 32],
                          e[32 * a:32 * a + 32, :, 32 * d:32 * d + 32]).then_inc(S["tr%d" % s], 1)
 
+    def spin():
+        ve.wait_ge(S.ex1, 1)
+        for b in range(4):
+            ve.transpose(T.et1[:, :, 32 * b:32 * b + 32], T.e1[:, b, :, :]).then_inc(S.tr1, 1)
+
     def weave(s):
         if s == 0:
             ve.wait_ge(S.e20_set, 1)
-        ve.wait_ge(S["tr%d" % s], 16)
+        if s == 1:
+            ve.wait_ge(S.xd, 16 * 16)
+        else:
+            ve.wait_ge(S["tr%d" % s], 16)
         for b in range(4):
-            ve.tensor_scalar(T["tile%d" % s][:, b:512:4], T["pt%d" % s][:, b, :], T.e20[:, 0:1], None,
+            src = T.pt1[:, :, 32 * b:32 * b + 32] if s == 1 else T["pt%d" % s][:, b, :]
+            ve.tensor_scalar(T["tile%d" % s][:, b:512:4], src, T.e20[:, 0:1], None,
                              AluOpType.max).then_inc(S["il%d" % s], 1)
 
     def pack(s):
@@ -214,29 +227,28 @@ def rank_program(g, core, T, topo):
     top(0)
     shift(0)
     turn(0, 0, 16)
-    weave(0)
-    pack(0)
-    top(2)
-    shift(2)
     top(1)
     shift(1)
-    turn(2, 0, 8)
+    top(2)
+    weave(0)
+    shift(2)
+    pack(0)
+    spin()
     top(3)
-    turn(2, 8, 12)
+    turn(2, 0, 2)
     shift(3)
-    turn(2, 12, 16)
-    turn(1, 0, 4)
+    turn(2, 2, 16)
+    turn(3, 0, 2)
     weave(2)
-    turn(1, 4, 6)
+    turn(3, 2, 4)
     pack(2)
-    turn(3, 0, 16)
-    turn(1, 6, 10)
+    turn(3, 4, 16)
     weave(3)
-    turn(1, 10, 12)
     pack(3)
-    turn(1, 12, 16)
     weave(1)
     pack(1)
+    ve.wait_ge(S.mmA1, 1)
+    ve.tensor_copy(T.snd1[:, 0:129], T.A[:, 512:641]).then_inc(S.ac1, 1)
 
     def w(s):
         return T.cw[:, 4 + order[s]:5 + order[s]]
@@ -275,49 +287,82 @@ def rank_program(g, core, T, topo):
     ve.wait_ge(S.us0, 1)
     ve.wait_ge(S.us2, 1)
     ve.tensor_tensor(T.acc1[:], u(0), u(2), AluOpType.add).then_inc(S.accs, 1)
+
     ve.wait_ge(S.a_in3, an[3])
     ve.wait_ge(S.dens, 2)
     ve.tensor_scalar(T.den[:, 2:3], tot(3), w(3), T.den[:, 1:2], AluOpType.mult, AluOpType.add).then_inc(S.dens, 1)
+    ve.wait_ge(S.a_in1, an[1])
+    ve.wait_ge(S.dens, 3)
+    ve.tensor_scalar(T.den[:, 3:4], tot(1), w(1), T.den[:, 2:3], AluOpType.mult, AluOpType.add).then_inc(S.dens, 1)
     ve.wait_ge(S.us3, 1)
     ve.wait_ge(S.accs, 1)
     ve.tensor_tensor(T.acc2[:], T.acc1[:], u(3), AluOpType.add).then_inc(S.accs, 1)
-
-    ve.wait_ge(S.dens, 3)
-    ve.wait_ge(S.a_in1, an[1])
-    ve.tensor_scalar(T.den[:, 3:4], tot(1), w(1), T.den[:, 2:3], AluOpType.mult, AluOpType.add).then_inc(S.dens, 1)
     ve.wait_ge(S.dens, 4)
     ve.reciprocal(T.rd[:], T.den[:, 3:4]).then_inc(S.rds, 1)
     ve.wait_ge(S.us1, 1)
     ve.wait_ge(S.accs, 2)
-    ve.tensor_tensor(T.acc3[:], T.acc2[:], u(1), AluOpType.add).then_inc(S.accs, 1)
+    for h in (1, 0):
+        ve.tensor_tensor(T.acc3[:, 64 * h:64 * h + 64], T.acc2[:, 64 * h:64 * h + 64], T.u[:, 128 + 64 * h:192 + 64 * h],
+                         AluOpType.add).then_inc(S["ah%d" % h], 1)
     ve.wait_ge(S.rds, 1)
-    ve.wait_ge(S.accs, 3)
-    ve.tensor_scalar(T.ot[:], T.acc3[:], T.rd[:], None, AluOpType.mult).then_inc(S.ots, 1)
-    ve.wait_ge(S.ots, 1)
-    ve.transpose(T.oh[:], T.ot[:, 64:128]).then_inc(S.ohs, 1)
-    for d in (0, 1):
-        for a in range(4):
-            ve.transpose(T.of[32 * d:32 * d + 32, 32 * a:32 * a + 32],
-                         T.ot[32 * a:32 * a + 32, 32 * d:32 * d + 32]).then_inc(S.ofv, 1)
-    sc.wait_ge(S.ohs, 1)
-    for d in (2, 3):
-        for a in range(4):
-            sc.activation(T.of[32 * d:32 * d + 32, 32 * a:32 * a + 32],
-                          T.oh[32 * a:32 * a + 32, 32 * (d - 2):32 * (d - 2) + 32], ACT.Copy).then_inc(S.ofa, 1)
+    ve.wait_ge(S.ah1, 1)
+    ve.tensor_scalar(T.ot[:, 64:128], T.acc3[:, 64:128], T.rd[:], None, AluOpType.mult).then_inc(S.ots, 1)
+    ve.wait_ge(S.ah0, 1)
+    ve.tensor_scalar(T.ot[:, 0:64], T.acc3[:, 0:64], T.rd[:], None, AluOpType.mult).then_inc(S.ota, 1)
+    for h in (1, 0):
+        if h:
+            ve.wait_ge(S.ots, 1)
+        else:
+            ve.wait_ge(S.ota, 1)
+        for a in (0, 1):
+            ve.transpose(T.oh[64 * h:64 * h + 64, a, :], T.ot[64 * a:64 * a + 64, 64 * h:64 * h + 64]).then_inc(S["oh%d" % h], 1)
 
-    for s in (0, 2, 3):
+    def piece(h, i, k):
+        return (T.of[64 * h + 32 * i:64 * h + 32 * i + 32, :, k, :],
+                T.oh[64 * h + 32 * k:64 * h + 32 * k + 32, :, 32 * i:32 * i + 32])
+
+    sc.wait_ge(S.oh1, 2)
+    for i, k in ((0, 0), (0, 1)):
+        out, in_ = piece(1, i, k)
+        sc.activation(out, in_, ACT.Copy).then_inc(S.oa1, 1)
+    sc.wait_ge(S.oh0, 2)
+    out, in_ = piece(0, 1, 1)
+    sc.activation(out, in_, ACT.Copy).then_inc(S.oa0, 1)
+    ve.wait_ge(S.oh1, 2)
+    for i, k in ((1, 0), (1, 1)):
+        out, in_ = piece(1, i, k)
+        ve.tensor_copy(out, in_).then_inc(S.of1, 1)
+    ve.wait_ge(S.oh0, 2)
+    for i, k in ((0, 0), (0, 1), (1, 0)):
+        out, in_ = piece(0, i, k)
+        ve.tensor_copy(out, in_).then_inc(S.of0, 1)
+
+    sy.wait_ge(S.q_in3, qn[3])
+    sy.dma_start(T.vo[:, 0:128].bitcast(dt.uint8), T.vc[:]).then_inc(S.ldv, 16)
+    sy.dma_start(T.vos[:, 0:128], T.vs[:]).then_inc(S.ldvs, 16)
+    sy.wait_ge(S.tr1, 4)
+    for d in range(4):
+        for a in range(4):
+            sy.dma_start(T.pt1[32 * d:32 * d + 32, a, :], T.et1[32 * a:32 * a + 32, d, :]).then_inc(S.xd, 16)
+    sy.wait_ge(S.a_in2, an[2])
+    for s in (0, 2):
         sy.wait_ge(S["il%d" % s], 4)
         sy.dma_start(T.p[order[s]], T["tile%d" % s][:]).then_inc(S.stp, 16)
     sy.wait_ge(S.cwts, 4)
     sy.dma_start(T.c[:], T.cwt[0:4, :]).then_inc(S.stc, 16)
     sy.dma_start(T.w[:], T.cwt[4:8, :]).then_inc(S.stc, 16)
+    sy.wait_ge(S.a_in3, an[3])
+    sy.wait_ge(S.il3, 4)
+    sy.dma_start(T.p[order[3]], T.tile3[:]).then_inc(S.stp, 16)
     sy.wait_ge(S.a_in1, an[1])
     sy.wait_ge(S.il1, 4)
     sy.dma_start(T.p[order[1]], T.tile1[:]).then_inc(S.stp, 16)
-    sy.wait_ge(S.ofv, 8)
-    sy.dma_start(T.o[0:64, :], T.of[0:64, :]).then_inc(S.sto, 16)
-    sc.wait_ge(S.ofa, 8)
-    sc.dma_start(T.o[64:128, :], T.of[64:128, :]).then_inc(S.sto2, 16)
+    sy.wait_ge(S.of1, 2)
+    sy.wait_ge(S.oa1, 2)
+    sy.dma_start(T.o[64:128, :], T.of[64:128, :, :, :]).then_inc(S.sto, 16)
+    sc.wait_ge(S.of0, 3)
+    sc.wait_ge(S.oa0, 1)
+    sc.dma_start(T.o[0:64, :], T.of[0:64, :, :, :]).then_inc(S.sto2, 16)
     sc.wait_ge(S.sto2, 16)
     sy.wait_ge(S.stp, 64)
     sy.wait_ge(S.stc, 32)

from concourse.bass import DstId, RemoteDMATransfer
from concourse.mybir import dt, AluOpType, AxisListType, ActivationFunctionType

N = 4
W = 132
SCALE = 0.0125
F8 = "float8_e4m3fn_x4"

SCRATCH = {
    "qin": ("sbuf", [128, 512], "bfloat16"),
    "ones": ("sbuf", [128, 512], "bfloat16"),
    "kcs": ("sbuf", [128, 512], F8),
    "kss": ("sbuf", [128, 512], "uint8"),
    "vo": ("sbuf", [128, 256], F8),
    "vos": ("sbuf", [128, 256], "uint8"),
    "nm": ("sbuf", [128, 4], "float32"),
    "nc": ("sbuf", [128, 4], "float32"),
    "m20": ("sbuf", [128, 1], "float32"),
    "e20": ("sbuf", [128, 1], "bfloat16"),
    "rcv": ("sbuf", [128, N * W], "float32"),
    "cw": ("sbuf", [128, 32], "float32"),
    "cwt": ("sbuf", [32, 128], "float32"),
    "low": ("sbuf", [128, 1], "float32"),
    "den": ("sbuf", [128, 4], "float32"),
    "rd": ("sbuf", [128, 1], "float32"),
    "u": ("sbuf", [128, 512], "float32"),
    "acc1": ("sbuf", [128, 128], "float32"),
    "acc2": ("sbuf", [128, 128], "float32"),
    "acc3": ("sbuf", [128, 128], "float32"),
    "ot": ("sbuf", [128, 128], "float32"),
    "oh": ("sbuf", [128, 2, 64], "float32"),
    "of": ("sbuf", [128, 2, 2, 32], "float32"),
    "e1": ("sbuf", [128, 4, 4, 32], "bfloat16"),
    "et1": ("sbuf", [128, 4, 128], "bfloat16"),
    "pt1": ("sbuf", [128, 4, 128], "bfloat16"),
    "S": ("psum", [128, 2048], "float32"),
    "A": ("psum", [128, 2048], "float32"),
}
SEMAPHORES = ["ldq", "ldk", "ldks", "ldv", "ldvs", "ones_set", "m20_set", "cw_set", "e20_set", "qq", "oneq", "loc", "locm",
              "c1", "c3", "stp", "stc", "sto", "sto2", "cpos", "lows", "ws", "dens", "accs", "ah0", "ah1", "cwts", "rds", "ots",
              "ota", "xd", "oh0", "oh1", "of0", "of1", "oa0", "oa1"]
for _s in range(N):
    if _s != 1:
        SCRATCH["e%d" % _s] = ("sbuf", [128, 4, 128], "bfloat16")
        SCRATCH["pt%d" % _s] = ("sbuf", [128, 4, 128], "bfloat16")
    SCRATCH["tile%d" % _s] = ("sbuf", [128, 512], "bfloat16")
    SCRATCH["qc%d" % _s] = ("sbuf", [128, 128], F8)
    SCRATCH["qs%d" % _s] = ("sbuf", [128, 128], "uint8")
    SCRATCH["pc%d" % _s] = ("sbuf", [128, 128], F8)
    SCRATCH["ps%d" % _s] = ("sbuf", [128, 128], "uint8")
    if _s:
        SCRATCH["snd%d" % _s] = ("sbuf", [128, W], "float32")
    SEMAPHORES += ["%s%d" % (_n, _s) for _n in ("q_in", "a_in", "mmS", "mmA", "red", "neg", "ex", "tr", "il", "qt", "ac", "us")]


def rank_program(g, core, T, topo):
    me = T.rank_of(core)
    if me is None:
        return
    ACT = ActivationFunctionType
    X = AxisListType.X
    S = T.sem
    ve, te, sc, sy = g.vector, g.tensor, g.scalar, g.sync
    cores = list(T.cores)

    def near(c):
        return (topo.host(c), topo.chip(c)) == (topo.host(core), topo.chip(core))

    order = sorted(range(N), key=lambda r: (r != me, not near(cores[r]), topo.die(cores[r]) != topo.die(core)))
    dst = [cores[r] for r in order]
    full = [0] + [topo.mask(core, d) for d in dst[1:]]
    away = full[2]
    here = full[1] & ~away

    def count(m):
        return bin(m).count("1")

    def did(d):
        rid, pid = topo.addr(d, core)
        return DstId(rid=rid, pnc=pid)

    def move(s, out, in_, sem, mask):
        return RemoteDMATransfer(src=in_, dst=out, dst_ids=[did(dst[s])], dma_engine_mask=mask, remote_sem=sem)

    def codes(t):
        return t[:].bitcast(dt.uint8)

    def slot(s):
        return order[s] * W

    def neg(s):
        return T.nc[:, order[s]:order[s] + 1]

    sy.dma_start(T.qin[:], T.q[:]).then_inc(S.ldq, 16)
    sc.dma_start(T.kcs[:].bitcast(dt.uint8), T.kc[:]).then_inc(S.ldk, 16)
    sy.dma_start(T.kss[:], T.ks[:]).then_inc(S.ldks, 16)

    nloc = {"q": 0, "m": 0}

    def sent(transfers, masks, kind="m"):
        g.remote_dma_fused(transfers, local_sem=S.loc if kind == "q" else S.locm)
        nloc[kind] += sum(count(t) for t in masks)

    g.wait_ge(S.qq, 1)
    sent([move(2, codes(T.qc2), codes(T.qc0), S.q_in2, away)], [away], "q")
    sent([move(1, codes(T.qc1), codes(T.qc0), S.q_in1, here)], [here], "q")
    sent([move(2, T.qs2[:], T.qs0[:], S.q_in2, away), move(1, T.qs1[:], T.qs0[:], S.q_in1, here)], [away, here], "q")
    sent([move(3, codes(T.qc3), codes(T.qc0), S.q_in3, away)], [away], "q")
    sent([move(3, T.qs3[:], T.qs0[:], S.q_in3, away)], [away], "q")
    mine = me * W
    g.wait_ge(S.neg1, 1)
    g.wait_ge(S.neg3, 1)
    cme = T.rcv[:, mine + 129:mine + 130]
    sent([move(3, cme, neg(3), S.c3, away), move(1, cme, neg(1), S.c1, here)], [away, here])
    g.wait_ge(S.ac2, 2)
    sent([move(2, T.rcv[:, mine:mine + 130], T.snd2[:, 0:130], S.a_in2, away)], [away])
    g.wait_ge(S.ac3, 1)
    sent([move(3, T.rcv[:, mine:mine + 129], T.snd3[:, 0:129], S.a_in3, away)], [away])
    g.wait_ge(S.ac1, 1)
    sent([move(1, T.rcv[:, mine:mine + 129], T.snd1[:, 0:129], S.a_in1, here)], [here])
    g.wait_ge(S.loc, nloc["q"])
    g.wait_ge(S.locm, nloc["m"])
    qn = [0, 2 * count(here), 2 * count(away), 2 * count(away)]
    an = [0, count(here), count(away), count(away)]

    def scores(s):
        if s:
            te.wait_ge(S["q_in%d" % s], qn[s])
        else:
            te.wait_ge(S.qq, 1)
            te.wait_ge(S.ldk, 16)
            te.wait_ge(S.ldks, 16)
        te.matmul_mx(T.S[:, 512 * s:512 * s + 512], T["qc%d" % s][:], T["qs%d" % s][:], T.kcs[:], T.kss[:],
                     True, True).then_inc(S["mmS%d" % s], 1)

    def values(s):
        if s == 0:
            te.wait_ge(S.oneq, 1)
            te.wait_ge(S.ldv, 16)
            te.wait_ge(S.ldvs, 16)
        te.wait_ge(S["qt%d" % s], 1)
        te.matmul_mx(T.A[:, 512 * s:512 * s + 256], T["pc%d" % s][:], T["ps%d" % s][:], T.vo[:], T.vos[:],
                     True, True).then_inc(S["mmA%d" % s], 1)

    scores(0)
    scores(1)
    scores(2)
    scores(3)
    values(0)
    values(2)
    values(3)
    values(1)

    def expo(s):
        sc.wait_ge(S["neg%d" % s], 1)
        sc.activation(T["e%d" % s][:], T.S[:, 512 * s:512 * s + 512], ACT.Exp, bias=neg(s),
                      scale=SCALE).then_inc(S["ex%d" % s], 1)

    def leave(s):
        sc.wait_ge(S["mmA%d" % s], 1)
        out = T["snd%d" % s][:, 0:129] if s else T.rcv[:, slot(0):slot(0) + 129]
        sc.activation(out, T.A[:, 512 * s:512 * s + 129], ACT.Copy).then_inc(S["ac%d" % s], 1)

    sc.wait_ge(S.m20_set, 1)
    sc.activation(T.e20[:], T.m20[:], ACT.Exp).then_inc(S.e20_set, 1)
    expo(0)
    sc.activation(T.rcv[:, slot(0) + 129:slot(0) + 130], neg(0), ACT.Copy).then_inc(S.ac0, 1)
    expo(1)
    expo(2)
    sc.activation(T.snd2[:, 129:130], neg(2), ACT.Copy).then_inc(S.ac2, 1)
    expo(3)
    leave(2)
    leave(3)
    leave(0)
    sc.wait_ge(S.cw_set, 1)
    sc.activation(T.cw[:, 0:4], T.nc[:, 0:4], ACT.Copy, scale=-1.0).then_inc(S.cpos, 1)

    ve.memset(T.m20[:], -20.0).then_inc(S.m20_set, 1)
    ve.memset(T.ones[:], 1.0).then_inc(S.ones_set, 1)
    ve.memset(T.cw[:], 0.0).then_inc(S.cw_set, 1)
    ve.wait_ge(S.ldq, 16)
    ve.quantize_mx(T.qc0[:], T.qs0[:], T.qin[:]).then_inc(S.qq, 1)
    ve.wait_ge(S.ones_set, 1)
    ve.quantize_mx(T.vo[:, 128:256], T.vos[:, 128:256], T.ones[:]).then_inc(S.oneq, 1)

    def top(s):
        r = order[s]
        ve.wait_ge(S["mmS%d" % s], 1)
        ve.tensor_reduce(T.nm[:, r:r + 1], T.S[:, 512 * s:512 * s + 512], X, AluOpType.max,
                         negate=True).then_inc(S["red%d" % s], 1)

    def shift(s):
        r = order[s]
        ve.wait_ge(S["red%d" % s], 1)
        ve.tensor_scalar(neg(s), T.nm[:, r:r + 1], SCALE, None, AluOpType.mult).then_inc(S["neg%d" % s], 1)

    def turn(s, lo, hi):
        e, p = T["e%d" % s], T["pt%d" % s]
        if lo == 0:
            ve.wait_ge(S["ex%d" % s], 1)
        for x in range(lo, hi):
            d, a = x // 4, x % 4
            ve.transpose(p[32 * d:32 * d + 32, :, 32 * a:32 * a + 32],
                         e[32 * a:32 * a + 32, :, 32 * d:32 * d + 32]).then_inc(S["tr%d" % s], 1)

    def spin():
        ve.wait_ge(S.ex1, 1)
        for b in range(4):
            ve.transpose(T.et1[:, :, 32 * b:32 * b + 32], T.e1[:, b, :, :]).then_inc(S.tr1, 1)

    def weave(s):
        if s == 0:
            ve.wait_ge(S.e20_set, 1)
        if s == 1:
            ve.wait_ge(S.xd, 16 * 16)
        else:
            ve.wait_ge(S["tr%d" % s], 16)
        for b in range(4):
            src = T.pt1[:, :, 32 * b:32 * b + 32] if s == 1 else T["pt%d" % s][:, b, :]
            ve.tensor_scalar(T["tile%d" % s][:, b:512:4], src, T.e20[:, 0:1], None,
                             AluOpType.max).then_inc(S["il%d" % s], 1)

    def pack(s):
        ve.wait_ge(S["il%d" % s], 4)
        ve.quantize_mx(T["pc%d" % s][:], T["ps%d" % s][:], T["tile%d" % s][:]).then_inc(S["qt%d" % s], 1)

    top(0)
    shift(0)
    turn(0, 0, 16)
    top(1)
    shift(1)
    top(2)
    weave(0)
    shift(2)
    pack(0)
    spin()
    top(3)
    turn(2, 0, 2)
    shift(3)
    turn(2, 2, 16)
    turn(3, 0, 2)
    weave(2)
    turn(3, 2, 4)
    pack(2)
    turn(3, 4, 16)
    weave(3)
    pack(3)
    weave(1)
    pack(1)
    ve.wait_ge(S.mmA1, 1)
    ve.tensor_copy(T.snd1[:, 0:129], T.A[:, 512:641]).then_inc(S.ac1, 1)

    def w(s):
        return T.cw[:, 4 + order[s]:5 + order[s]]

    def arr(s):
        return T.rcv[:, slot(s):slot(s) + 128]

    def tot(s):
        return T.rcv[:, slot(s) + 128:slot(s) + 129]

    def u(s):
        return T.u[:, 128 * s:128 * s + 128]

    shifts = T.rcv[:, 129:N * W:W]
    ve.wait_ge(S.c1, count(here))
    ve.wait_ge(S.c3, count(away))
    ve.wait_ge(S.ac0, 2)
    ve.wait_ge(S.a_in2, an[2])
    ve.tensor_reduce(T.low[:], shifts, X, AluOpType.min).then_inc(S.lows, 1)

    sc.wait_ge(S.lows, 1)
    sc.activation(T.cw[:, 4:8], shifts, ACT.Exp, bias=T.low[:], scale=-1.0).then_inc(S.ws, 1)
    sc.wait_ge(S.ws, 1)
    for s in (0, 2, 3, 1):
        if s in (1, 3):
            sc.wait_ge(S["a_in%d" % s], an[s])
        sc.activation(u(s), arr(s), ACT.Identity, scale=w(s)).then_inc(S["us%d" % s], 1)

    ve.wait_ge(S.ws, 1)
    ve.tensor_scalar(T.den[:, 0:1], tot(0), w(0), None, AluOpType.mult).then_inc(S.dens, 1)
    ve.wait_ge(S.cpos, 1)
    for a in range(4):
        ve.transpose(T.cwt[0:32, 32 * a:32 * a + 32], T.cw[32 * a:32 * a + 32, 0:32]).then_inc(S.cwts, 1)
    ve.wait_ge(S.dens, 1)
    ve.tensor_scalar(T.den[:, 1:2], tot(2), w(2), T.den[:, 0:1], AluOpType.mult, AluOpType.add).then_inc(S.dens, 1)
    ve.wait_ge(S.us0, 1)
    ve.wait_ge(S.us2, 1)
    ve.tensor_tensor(T.acc1[:], u(0), u(2), AluOpType.add).then_inc(S.accs, 1)

    ve.wait_ge(S.a_in3, an[3])
    ve.wait_ge(S.dens, 2)
    ve.tensor_scalar(T.den[:, 2:3], tot(3), w(3), T.den[:, 1:2], AluOpType.mult, AluOpType.add).then_inc(S.dens, 1)
    ve.wait_ge(S.a_in1, an[1])
    ve.wait_ge(S.dens, 3)
    ve.tensor_scalar(T.den[:, 3:4], tot(1), w(1), T.den[:, 2:3], AluOpType.mult, AluOpType.add).then_inc(S.dens, 1)
    ve.wait_ge(S.us3, 1)
    ve.wait_ge(S.accs, 1)
    ve.tensor_tensor(T.acc2[:], T.acc1[:], u(3), AluOpType.add).then_inc(S.accs, 1)
    ve.wait_ge(S.dens, 4)
    ve.reciprocal(T.rd[:], T.den[:, 3:4]).then_inc(S.rds, 1)
    ve.wait_ge(S.us1, 1)
    ve.wait_ge(S.accs, 2)
    for h in (1, 0):
        ve.tensor_tensor(T.acc3[:, 64 * h:64 * h + 64], T.acc2[:, 64 * h:64 * h + 64], T.u[:, 128 + 64 * h:192 + 64 * h],
                         AluOpType.add).then_inc(S["ah%d" % h], 1)
    ve.wait_ge(S.rds, 1)
    ve.wait_ge(S.ah1, 1)
    ve.tensor_scalar(T.ot[:, 64:128], T.acc3[:, 64:128], T.rd[:], None, AluOpType.mult).then_inc(S.ots, 1)
    ve.wait_ge(S.ah0, 1)
    ve.tensor_scalar(T.ot[:, 0:64], T.acc3[:, 0:64], T.rd[:], None, AluOpType.mult).then_inc(S.ota, 1)
    for h in (1, 0):
        if h:
            ve.wait_ge(S.ots, 1)
        else:
            ve.wait_ge(S.ota, 1)
        for a in (0, 1):
            ve.transpose(T.oh[64 * h:64 * h + 64, a, :], T.ot[64 * a:64 * a + 64, 64 * h:64 * h + 64]).then_inc(S["oh%d" % h], 1)

    def piece(h, i, k):
        return (T.of[64 * h + 32 * i:64 * h + 32 * i + 32, :, k, :],
                T.oh[64 * h + 32 * k:64 * h + 32 * k + 32, :, 32 * i:32 * i + 32])

    sc.wait_ge(S.oh1, 2)
    for i, k in ((0, 0), (0, 1)):
        out, in_ = piece(1, i, k)
        sc.activation(out, in_, ACT.Copy).then_inc(S.oa1, 1)
    sc.wait_ge(S.oh0, 2)
    out, in_ = piece(0, 1, 1)
    sc.activation(out, in_, ACT.Copy).then_inc(S.oa0, 1)
    ve.wait_ge(S.oh1, 2)
    for i, k in ((1, 0), (1, 1)):
        out, in_ = piece(1, i, k)
        ve.tensor_copy(out, in_).then_inc(S.of1, 1)
    ve.wait_ge(S.oh0, 2)
    for i, k in ((0, 0), (0, 1), (1, 0)):
        out, in_ = piece(0, i, k)
        ve.tensor_copy(out, in_).then_inc(S.of0, 1)

    sy.wait_ge(S.q_in3, qn[3])
    sy.dma_start(T.vo[:, 0:128].bitcast(dt.uint8), T.vc[:]).then_inc(S.ldv, 16)
    sy.dma_start(T.vos[:, 0:128], T.vs[:]).then_inc(S.ldvs, 16)
    sy.wait_ge(S.tr1, 4)
    for d in range(4):
        for a in range(4):
            sy.dma_start(T.pt1[32 * d:32 * d + 32, a, :], T.et1[32 * a:32 * a + 32, d, :]).then_inc(S.xd, 16)
    sy.wait_ge(S.a_in2, an[2])
    for s in (0, 2):
        sy.wait_ge(S["il%d" % s], 4)
        sy.dma_start(T.p[order[s]], T["tile%d" % s][:]).then_inc(S.stp, 16)
    sy.wait_ge(S.cwts, 4)
    sy.dma_start(T.c[:], T.cwt[0:4, :]).then_inc(S.stc, 16)
    sy.dma_start(T.w[:], T.cwt[4:8, :]).then_inc(S.stc, 16)
    sy.wait_ge(S.a_in3, an[3])
    sy.wait_ge(S.il3, 4)
    sy.dma_start(T.p[order[3]], T.tile3[:]).then_inc(S.stp, 16)
    sy.wait_ge(S.a_in1, an[1])
    sy.wait_ge(S.il1, 4)
    sy.dma_start(T.p[order[1]], T.tile1[:]).then_inc(S.stp, 16)
    sy.wait_ge(S.of1, 2)
    sy.wait_ge(S.oa1, 2)
    sy.dma_start(T.o[64:128, :], T.of[64:128, :, :, :]).then_inc(S.sto, 16)
    sc.wait_ge(S.of0, 3)
    sc.wait_ge(S.oa0, 1)
    sc.dma_start(T.o[0:64, :], T.of[0:64, :, :, :]).then_inc(S.sto2, 16)
    sc.wait_ge(S.sto2, 16)
    sy.wait_ge(S.stp, 64)
    sy.wait_ge(S.stc, 32)
    sy.wait_ge(S.sto, 16)
